import numpy as np
import ml_dtypes


def mxq(x, axis, fmt="e4m3"):
    dtype, down = {"e4m3": (ml_dtypes.float8_e4m3fn, 7), "e5m2": (ml_dtypes.float8_e5m2, 14)}[fmt]
    v = np.moveaxis(np.asarray(x, np.float32).astype(ml_dtypes.bfloat16).astype(np.float64), axis, -1)
    blocks = v.reshape(v.shape[:-1] + (-1, 32))
    amax = np.abs(blocks).max(-1, keepdims=True)
    byte = np.maximum(np.where(amax > 0, np.frexp(amax)[1] - 1 + 127, 0) - down, 1)
    scale = np.exp2(byte - 127.0)
    codes = (blocks / scale).astype(np.float32).astype(dtype).astype(np.float64)
    return np.moveaxis((codes * scale).reshape(v.shape), -1, axis)


WIDE = False


def mx_kscale(k):
    if not WIDE:
        return np.ones(k)
    levels = np.array([10, -10, 5, -5, 0])
    if k % 512:
        return np.exp2(np.random.permutation(np.resize(levels, k // 32))).repeat(32)
    a = np.empty((k // 512, 16))
    for p in range(k // 512):
        a[p, :8] = np.random.permutation(np.resize(levels, 8))
        for g in range(8):
            far = levels[np.abs(levels - a[p, g]) >= 10]
            a[p, g + 8] = far[np.random.randint(len(far))]
    return np.exp2(a.ravel()).repeat(32)


def f64(x):
    return np.asarray(x).astype(np.float64)


def striped(idx):
    return np.tile(idx.reshape(-1, 16).T, (8, 1)).astype(np.uint16)


def unstriped(offs):
    return offs[:16].T.reshape(-1).astype(np.int64)


def striped8(idx):
    return np.concatenate([x.reshape(-1, 16).T for x in idx]).astype(np.uint16)


def runs(offs, k):
    lists = np.stack([offs[16 * r : 16 * r + 16].T.reshape(-1) for r in range(8)]).astype(np.int64)
    return lists[np.arange(k) % 512 // 64]


def pack_weight(w):
    k, n = w.shape
    w = f64(np.asarray(w, np.float32).astype(ml_dtypes.bfloat16)).reshape(k // 32, 32, n)
    amax = np.abs(w).max(1)
    byte = np.clip(np.where(amax > 0, np.frexp(amax)[1] - 1 + 127 - 7, 1), 1, 254)
    scaled = (w * np.exp2(127.0 - byte)[:, None, :]).reshape(k, n).astype(np.float32)
    words = np.ascontiguousarray(scaled.reshape(k // 512, 128, 4, n).transpose(0, 1, 3, 2)).astype(ml_dtypes.float8_e4m3fn).view(np.uint8)
    return words, np.ascontiguousarray(byte.astype(np.uint8).reshape(k // 512, 16, n))


def unpack_weight(words, scales):
    g, p, n, _ = words.shape
    vals = np.ascontiguousarray(words).view(ml_dtypes.float8_e4m3fn).astype(np.float64) * np.repeat(np.exp2(scales.astype(np.float64) - 127.0), 8, axis=1)[..., None]
    return vals.transpose(0, 1, 3, 2).reshape(g * 512, n)


K, T, S, H, G = 512, 1024, 512, 512, 2048


def setup_inputs():
    n = np.random.standard_normal
    s = mx_kscale(K)[:, None]
    packed_xT = pack_weight(n((K, T)) * s)
    packed_dT = pack_weight(n((K, G)) / s)
    return {
        "x_words": packed_xT[0],
        "x_scales": packed_xT[1],
        "w1": (n((K, H)) / np.sqrt(K) / s).astype(np.float32),
        "w2": (n((K, H)) / np.sqrt(K) / s).astype(np.float32),
        "gs": (np.random.uniform(0.5, 1.5, (K, 1)) * s).astype(np.float32),
        "d_words": packed_dT[0],
        "d_scales": packed_dT[1],
        "offs": striped(np.random.permutation(T)[:S]),
        "two": striped(np.random.permutation(T)[:S]),
        "n1": striped8(np.stack([np.random.permutation(S) for _ in range(8)])),
        "n2": striped8(np.stack([np.random.permutation(S) for _ in range(8)])),
        "k1": striped8(np.random.randint(0, G, (8, H))),
        "n3": striped8(np.stack([np.random.permutation(S) for _ in range(8)])),
        "n4": striped8(np.stack([np.random.permutation(S) for _ in range(8)])),
        "n5": striped8(np.stack([np.random.permutation(S) for _ in range(8)])),
    }


def reference(x_words, x_scales, w1, w2, gs, d_words, d_scales, offs, two, n1, n2, k1, n3, n4, n5):
    d_k1 = unpack_weight(d_words, d_scales)[np.arange(K)[:, None], runs(k1, K)]
    xq = unpack_weight(x_words, x_scales)[:, unstriped(offs)]
    y = mxq(f64(w1), 0, "e4m3").T @ xq
    x_two = unpack_weight(x_words, x_scales)[:, unstriped(two)]
    d = mxq(f64(w2), 0, "e4m3").T @ x_two
    z = f64(gs) * (y[np.arange(H)[:, None], runs(n1, H)] - (np.tanh(d) * (d[np.arange(H)[:, None], runs(n2, H)])))
    h = 0.0625 * ((d_k1.T @ mxq(z, 0, "e4m3")))
    ex = np.exp(0.5 * h)
    return np.log((ex + ex[np.arange(H)[:, None], runs(n3, H)]) / (ex[np.arange(H)[:, None], runs(n4, H)] + ex[np.arange(H)[:, None], runs(n5, H)]))

@@ -1,0 +1,213 @@
+from contextlib import ExitStack
+
+import concourse.mybir as mybir
+
+F32 = mybir.dt.float32
+BF16 = mybir.dt.bfloat16
+U32 = mybir.dt.uint32
+I32 = mybir.dt.int32
+U16 = mybir.dt.uint16
+U8 = mybir.dt.uint8
+FP8X4 = mybir.dt.float8_e4m3fn_x4
+ACT = mybir.ActivationFunctionType
+ALU = mybir.AluOpType
+
+P = 128
+K, T, S, H, G = 512, 1024, 512, 512, 2048
+TILES = 4
+HALF = S // 2
+FLOPS = 3 * 2 * K * H * S
+EXP_SCALE = 0.5 * 0.0625
+SCALAR_GATHER_TILES = (1, 2, 3)
+Z_PIECES = ((0, 256), (256, 128), (384, 128))
+
+
+def tile_picked_twqsoftbodds_none_p_kernel(tc, x_words, x_scales, w1, w2, gs, d_words, d_scales, offs, two, n1, n2, k1, n3, n4, n5, out):
+    nc = tc.nc
+    with ExitStack() as ctx:
+        lists = ctx.enter_context(tc.tile_pool(name="lists", bufs=1))
+        keep = ctx.enter_context(tc.tile_pool(name="keep", bufs=1))
+        psum = ctx.enter_context(tc.psum_pool(name="psum", bufs=1))
+
+        def load_list(src, name):
+            t = lists.tile([P, S // 16], U16, name=name)
+            nc.sync.dma_start(t[:], src)
+            return t
+
+        def sb(shape, dtype, name):
+            return keep.tile(shape, dtype, name=name, align_bytes=64)
+
+        def load_weight_half(w, h, name):
+            raw = sb([P, 4, HALF], F32, name)
+            nc.sync.dma_start(raw[:], w.rearrange("(p j) c -> p j c", j=4)[:, :, h * HALF : (h + 1) * HALF])
+            return raw
+
+        def cols(h):
+            return slice(h * HALF, (h + 1) * HALF)
+
+        def entries(lst, h):
+            return lst[:, h * (HALF // 16) : (h + 1) * (HALF // 16)]
+
+        two_l = load_list(two, "two_l")
+        xs_tab = sb([P, T], U8, "xs_tab")
+        for q in range(4):
+            nc.sync.dma_start(
+                xs_tab[32 * q : 32 * q + 32, :].bitcast(I32),
+                x_scales[0, 4 * q : 4 * q + 4, :].bitcast(I32).unsqueeze(0).to_broadcast([8, 4, T // 4]),
+            )
+        xw_tab = sb([P, T], U32, "xw_tab")
+        nc.sync.dma_start(xw_tab[:].bitcast(I32), x_words[0].rearrange("p n t -> p (n t)").bitcast(I32))
+        offs_l = load_list(offs, "offs_l")
+        w2_raw = [load_weight_half(w2, 0, "w2_raw0")]
+        w2_raw.append(load_weight_half(w2, 1, "w2_raw1"))
+        gs_sb = sb([P, 4], F32, "gs_sb")
+        nc.sync.dma_start(gs_sb[:], gs.rearrange("(p t) o -> p (t o)", t=4))
+        n2_l = load_list(n2, "n2_l")
+        w1_raw = [load_weight_half(w1, 0, "w1_raw0")]
+        ds_tab = sb([P, G], U8, "ds_tab")
+        nc.sync.dma_start(ds_tab[:].bitcast(I32), d_scales[0].bitcast(I32).unsqueeze(1).to_broadcast([16, 8, G // 4]))
+        k1_l = load_list(k1, "k1_l")
+        w1_raw.append(load_weight_half(w1, 1, "w1_raw1"))
+        dw_tab = sb([P, G], U32, "dw_tab")
+        nc.sync.dma_start(dw_tab[:].bitcast(I32), d_words[0].rearrange("p n t -> p (n t)").bitcast(I32))
+        n1_l = load_list(n1, "n1_l")
+        n4_l = load_list(n4, "n4_l")
+        n5_l = load_list(n5, "n5_l")
+        n3_l = load_list(n3, "n3_l")
+
+        def gather(table, lst, dtype, name):
+            g = sb([P, S], dtype, name)
+            nc.vector.tensor_copy(g[:], table[:].indirect(lst[:]))
+            return g
+
+        def interleave_weight(raw, name):
+            grouped = sb([P, 4 * H], BF16, name)
+            view = grouped[:].rearrange("p (t m j) -> p m j t", t=4, j=4)
+            for h in range(2):
+                nc.scalar.copy(view[:, 64 * h : 64 * h + 64], raw[h][:].rearrange("p j (m t) -> p m j t", t=4))
+            return grouped
+
+        def quantize(src, width, name):
+            codes = sb([P, width], U32, name + "_codes")
+            scales = sb([P, width], U8, name + "_scales")
+            nc.vector.quantize_mx(out=codes[:].bitcast(FP8X4), scales=scales[:], in_=src[:])
+            return codes, scales
+
+        def product(bank, lhs, t, rhs):
+            m = slice(t * P, (t + 1) * P)
+            nc.tensor.matmul_mx(out=bank, lhsT=lhs[0][:, m].bitcast(FP8X4), lhsT_scale=lhs[1][:, m],
+                                rhs=rhs[0][:].bitcast(FP8X4), rhs_scale=rhs[1][:], start=True, stop=True)
+
+        xs_two = gather(xs_tab, two_l, U8, "xs_two")
+        xw_two = gather(xw_tab, two_l, U32, "xw_two")
+        w2_grouped = interleave_weight(w2_raw, "w2_grouped")
+        xs_idx = gather(xs_tab, offs_l, U8, "xs_idx")
+        xw_idx = gather(xw_tab, offs_l, U32, "xw_idx")
+        w2_q = quantize(w2_grouped, H, "w2")
+
+        tanh_d, d_sc = [], []
+        for t in range(TILES):
+            bank = psum.tile([P, S], F32, name=f"d_bank{t}", tag=f"first{t}")
+            product(bank[:], w2_q, t, (xw_two, xs_two))
+            td = sb([P, S], F32, f"tanh_d{t}")
+            nc.scalar.activation(td[:], bank[:], ACT.Tanh)
+            dd = sb([P, S], F32, f"d_sc{t}")
+            nc.scalar.activation(dd[:], bank[:], ACT.Copy, scale=gs_sb[:, t : t + 1])
+            tanh_d.append(td)
+            d_sc.append(dd)
+
+        ds_g = gather(ds_tab, k1_l, U8, "ds_g")
+        ds_dealt = sb([P, H], U8, "ds_dealt")
+        nc.vector.tensor_copy(ds_dealt[:].bitcast(I32).rearrange("p (t u) -> p u t", t=4),
+                              ds_g[:].bitcast(I32).rearrange("p (u t) -> p u t", t=4))
+        ds_placed = sb([P, H], U8, "ds_placed")
+        nc.gpsimd.memset(ds_placed[:], 0)
+        for q in range(4):
+            nc.sync.dma_start(ds_placed[32 * q : 32 * q + 4, :].bitcast(I32), ds_dealt[32 * q : 32 * q + 32 : 8, :].bitcast(I32))
+
+        w1_grouped = interleave_weight(w1_raw, "w1_grouped")
+
+        prod = []
+        for t in range(TILES):
+            m = sb([P, S], F32, f"prod{t}")
+            for h in range(2):
+                nc.vector.tensor_tensor(m[:, cols(h)], d_sc[t][:].indirect(entries(n2_l, h)), tanh_d[t][:, cols(h)], ALU.mult)
+            prod.append(m)
+            if t == 0:
+                w1_q = quantize(w1_grouped, H, "w1")
+
+        y_sc = []
+        for t in range(TILES):
+            bank = psum.tile([P, S], F32, name=f"y_bank{t}", tag=f"second{t}")
+            product(bank[:], w1_q, t, (xw_idx, xs_idx))
+            yy = sb([P, S], F32, f"y_sc{t}")
+            nc.scalar.activation(yy[:], bank[:], ACT.Copy, scale=gs_sb[:, t : t + 1])
+            y_sc.append(yy)
+
+        dw_g = gather(dw_tab, k1_l, U32, "dw_g")
+        dw_dealt = sb([P, H], U32, "dw_dealt")
+        nc.vector.tensor_copy(dw_dealt[:].rearrange("p (t u q) -> p u t q", t=4, q=4),
+                              dw_g[:].rearrange("p (u t q) -> p u t q", t=4, q=4))
+
+        ex = [sb([P, S], F32, f"ex{t}") for t in range(TILES)]
+        ex_twin = [sb([P, S], F32, f"ex_twin{t}") for t in range(TILES)]
+        h_sb = {t: sb([P, S], F32, f"h_sb{t}") for t in SCALAR_GATHER_TILES}
+        fourth = [sb([P, S], F32, f"fourth{t}") for t in range(TILES)]
+
+        z = [sb([P, 4, width], F32, f"z{i}") for i, (first, width) in enumerate(Z_PIECES)]
+        for i, (first, width) in enumerate(Z_PIECES):
+            for t in range(TILES):
+                nc.vector.tensor_tensor(z[i][:, t, :], y_sc[t][:].indirect(n1_l[:, first // 16 : (first + width) // 16]),
+                                        prod[t][:, first : first + width], ALU.subtract)
+        last = len(Z_PIECES) - 1
+        for i, (first, width) in enumerate(Z_PIECES):
+            piece = slice(first, first + width)
+            z_grouped = sb([P, 4 * width], BF16, f"z_grouped{i}")
+            dst = z_grouped[:].rearrange("p (c i t) -> p c t i", i=4, t=4)
+            src = z[i][:].rearrange("p t (c i) -> p c t i", i=4)
+            if i < last:
+                nc.scalar.copy(dst, src)
+            else:
+                nc.vector.tensor_copy(dst, src)
+            z_q = quantize(z_grouped, width, f"z{i}")
+            for t in range(TILES):
+                bank = psum.tile([P, width], F32, name=f"h_bank{i}{t}", tag=("first", "second")[i % 2] + f"{t}")
+                product(bank[:], (dw_dealt, ds_placed), t, z_q)
+                nc.scalar.activation(ex[t][:, piece], bank[:], ACT.Exp, scale=EXP_SCALE)
+                if i == last - 1:
+                    nc.sync.dma_start(ex_twin[t][:, : first + width], ex[t][:, : first + width])
+                if i == last:
+                    nc.sync.dma_start(ex_twin[t][:, piece], ex[t][:, piece])
+                if t in SCALAR_GATHER_TILES:
+                    nc.scalar.copy(h_sb[t][:, piece], bank[:])
+                    if i == last:
+                        for g in range(2):
+                            nc.scalar.activation(fourth[t][:, cols(g)], h_sb[t][:].indirect(entries(n4_l, g)), ACT.Exp, scale=EXP_SCALE)
+
+        sums = [sb([P, 2, S], F32, f"sums{t}") for t in range(TILES)]
+
+        def denominator(t):
+            if t not in SCALAR_GATHER_TILES:
+                for g in range(2):
+                    nc.vector.tensor_copy(fourth[t][:, cols(g)], ex[t][:].indirect(entries(n4_l, g)))
+            for g in range(2):
+                nc.vector.tensor_tensor(sums[t][:, 1, cols(g)], ex[t][:].indirect(entries(n5_l, g)), fourth[t][:, cols(g)], ALU.add)
+
+        def numerator(t):
+            for g in range(2):
+                nc.vector.tensor_tensor(sums[t][:, 0, cols(g)], ex[t][:].indirect(entries(n3_l, g)), ex_twin[t][:, cols(g)], ALU.add)
+
+        def finish(t):
+            logs = sb([P, 2, S], F32, f"logs{t}")
+            nc.scalar.activation(logs[:], sums[t][:], ACT.Ln)
+            res = sb([P, S], F32, f"res{t}")
+            nc.vector.tensor_tensor(res[:], logs[:, 0, :], logs[:, 1, :], ALU.subtract)
+            nc.sync.dma_start(out.rearrange("(u t q) n -> t u q n", t=4, q=4)[t], res[:])
+
+        denominator(0)
+        for t in range(TILES):
+            if t + 1 < TILES:
+                denominator(t + 1)
+            numerator(t)
+        for t in range(TILES):
+            finish(t)

@@ -18,7 +18,7 @@ TILES = 4
 HALF = S // 2
 FLOPS = 3 * 2 * K * H * S
 EXP_SCALE = 0.5 * 0.0625
-SCALAR_GATHER_TILES = (1, 2, 3)
+DIRECT_TWINS = 2
 Z_PIECES = ((0, 256), (256, 128), (384, 128))
 
 
@@ -34,12 +34,12 @@ def tile_picked_twqsoftbodds_none_p_kernel(tc, x_words, x_scales, w1, w2, gs, d_
             nc.sync.dma_start(t[:], src)
             return t
 
-        def sb(shape, dtype, name):
-            return keep.tile(shape, dtype, name=name, align_bytes=64)
+        def sb(shape, dtype, name, tag=None):
+            return keep.tile(shape, dtype, name=name, tag=tag or name, align_bytes=64)
 
         def load_weight_half(w, h, name):
-            raw = sb([P, 4, HALF], F32, name)
-            nc.sync.dma_start(raw[:], w.rearrange("(p j) c -> p j c", j=4)[:, :, h * HALF : (h + 1) * HALF])
+            raw = sb([P, 4 * HALF], F32, name)
+            nc.sync.dma_start(raw[:].rearrange("p (j c) -> p j c", j=4), w.rearrange("(p j) c -> p j c", j=4)[:, :, h * HALF : (h + 1) * HALF])
             return raw
 
         def cols(h):
@@ -48,22 +48,25 @@ def tile_picked_twqsoftbodds_none_p_kernel(tc, x_words, x_scales, w1, w2, gs, d_
         def entries(lst, h):
             return lst[:, h * (HALF // 16) : (h + 1) * (HALF // 16)]
 
-        two_l = load_list(two, "two_l")
         xs_tab = sb([P, T], U8, "xs_tab")
-        for q in range(4):
-            nc.sync.dma_start(
+
+        def load_x_scales(q):
+            (nc.sync, nc.scalar)[q // 2].dma_start(
                 xs_tab[32 * q : 32 * q + 32, :].bitcast(I32),
                 x_scales[0, 4 * q : 4 * q + 4, :].bitcast(I32).unsqueeze(0).to_broadcast([8, 4, T // 4]),
             )
+
+        two_l = load_list(two, "two_l")
+        for q in range(4):
+            load_x_scales(q)
         xw_tab = sb([P, T], U32, "xw_tab")
         nc.sync.dma_start(xw_tab[:].bitcast(I32), x_words[0].rearrange("p n t -> p (n t)").bitcast(I32))
         offs_l = load_list(offs, "offs_l")
-        w2_raw = [load_weight_half(w2, 0, "w2_raw0")]
-        w2_raw.append(load_weight_half(w2, 1, "w2_raw1"))
+        w2_raw = [load_weight_half(w2, h, f"w2_raw{h}") for h in range(2)]
+        w1_raw = [load_weight_half(w1, 0, "w1_raw0")]
         gs_sb = sb([P, 4], F32, "gs_sb")
         nc.sync.dma_start(gs_sb[:], gs.rearrange("(p t) o -> p (t o)", t=4))
         n2_l = load_list(n2, "n2_l")
-        w1_raw = [load_weight_half(w1, 0, "w1_raw0")]
         ds_tab = sb([P, G], U8, "ds_tab")
         nc.sync.dma_start(ds_tab[:].bitcast(I32), d_scales[0].bitcast(I32).unsqueeze(1).to_broadcast([16, 8, G // 4]))
         k1_l = load_list(k1, "k1_l")
@@ -80,17 +83,16 @@ def tile_picked_twqsoftbodds_none_p_kernel(tc, x_words, x_scales, w1, w2, gs, d_
             nc.vector.tensor_copy(g[:], table[:].indirect(lst[:]))
             return g
 
-        def interleave_weight(raw, name):
-            grouped = sb([P, 4 * H], BF16, name)
+        def interleave_half(grouped, raw, h):
             view = grouped[:].rearrange("p (t m j) -> p m j t", t=4, j=4)
-            for h in range(2):
-                nc.scalar.copy(view[:, 64 * h : 64 * h + 64], raw[h][:].rearrange("p j (m t) -> p m j t", t=4))
-            return grouped
+            nc.scalar.copy(view[:, 64 * h : 64 * h + 64], raw[h][:].rearrange("p (j m t) -> p m j t", j=4, t=4))
 
-        def quantize(src, width, name):
+        def quantize(src, width, name, calls=1):
             codes = sb([P, width], U32, name + "_codes")
             scales = sb([P, width], U8, name + "_scales")
-            nc.vector.quantize_mx(out=codes[:].bitcast(FP8X4), scales=scales[:], in_=src[:])
+            step = width // calls
+            for c in range(0, width, step):
+                nc.vector.quantize_mx(out=codes[:, c : c + step].bitcast(FP8X4), scales=scales[:, c : c + step], in_=src[:, 4 * c : 4 * (c + step)])
             return codes, scales
 
         def product(bank, lhs, t, rhs):
@@ -100,41 +102,51 @@ def tile_picked_twqsoftbodds_none_p_kernel(tc, x_words, x_scales, w1, w2, gs, d_
 
         xs_two = gather(xs_tab, two_l, U8, "xs_two")
         xw_two = gather(xw_tab, two_l, U32, "xw_two")
-        w2_grouped = interleave_weight(w2_raw, "w2_grouped")
+        w2_grouped = sb([P, 4 * H], BF16, "w2_grouped")
+        w1_grouped = sb([P, 4 * H], BF16, "w1_grouped")
+        interleave_half(w2_grouped, w2_raw, 0)
+        interleave_half(w2_grouped, w2_raw, 1)
+        interleave_half(w1_grouped, w1_raw, 0)
         xs_idx = gather(xs_tab, offs_l, U8, "xs_idx")
         xw_idx = gather(xw_tab, offs_l, U32, "xw_idx")
-        w2_q = quantize(w2_grouped, H, "w2")
-
-        tanh_d, d_sc = [], []
-        for t in range(TILES):
-            bank = psum.tile([P, S], F32, name=f"d_bank{t}", tag=f"first{t}")
-            product(bank[:], w2_q, t, (xw_two, xs_two))
-            td = sb([P, S], F32, f"tanh_d{t}")
-            nc.scalar.activation(td[:], bank[:], ACT.Tanh)
-            dd = sb([P, S], F32, f"d_sc{t}")
-            nc.scalar.activation(dd[:], bank[:], ACT.Copy, scale=gs_sb[:, t : t + 1])
-            tanh_d.append(td)
-            d_sc.append(dd)
+        w2_q = quantize(w2_grouped, H, "w2", calls=2)
 
         ds_g = gather(ds_tab, k1_l, U8, "ds_g")
         ds_dealt = sb([P, H], U8, "ds_dealt")
         nc.vector.tensor_copy(ds_dealt[:].bitcast(I32).rearrange("p (t u) -> p u t", t=4),
                               ds_g[:].bitcast(I32).rearrange("p (u t) -> p u t", t=4))
         ds_placed = sb([P, H], U8, "ds_placed")
-        nc.gpsimd.memset(ds_placed[:], 0)
+        nc.vector.memset(ds_placed[:].bitcast(I32), 0)
         for q in range(4):
             nc.sync.dma_start(ds_placed[32 * q : 32 * q + 4, :].bitcast(I32), ds_dealt[32 * q : 32 * q + 32 : 8, :].bitcast(I32))
 
-        w1_grouped = interleave_weight(w1_raw, "w1_grouped")
+        ex_window = [sb([P, 2 * S], F32, f"ex_window{t}") for t in range(TILES)]
+        ex = [w[:, :S] for w in ex_window]
+        tanh_d = [w1_raw[0][:, S:]] + [w[:, S:] for w in ex_window[1:]]
+        d_sc = [sb([P, S], F32, f"d_sc{t}") for t in range(TILES)]
+        d_banks = []
 
-        prod = []
+        def tanh_half(t, h):
+            nc.scalar.activation(tanh_d[t][:, cols(h)], d_banks[t][:, cols(h)], ACT.Tanh)
+
+        def times_lookup(dst, t, h):
+            nc.vector.tensor_tensor(dst, d_sc[t][:].indirect(entries(n2_l, h)), tanh_d[t][:, cols(h)], ALU.mult)
+
+        prod_a = [sb([P, HALF], F32, f"prod_a{t}") for t in range(TILES)]
         for t in range(TILES):
-            m = sb([P, S], F32, f"prod{t}")
-            for h in range(2):
-                nc.vector.tensor_tensor(m[:, cols(h)], d_sc[t][:].indirect(entries(n2_l, h)), tanh_d[t][:, cols(h)], ALU.mult)
-            prod.append(m)
+            d_banks.append(psum.tile([P, S], F32, name=f"d_bank{t}", tag=f"first{t}"))
+            product(d_banks[t][:], w2_q, t, (xw_two, xs_two))
+            tanh_half(t, 0)
+            nc.scalar.activation(d_sc[t][:], d_banks[t][:], ACT.Copy, scale=gs_sb[:, t : t + 1])
+            times_lookup(prod_a[t][:], t, 0)
             if t == 0:
+                interleave_half(w1_grouped, w1_raw, 1)
                 w1_q = quantize(w1_grouped, H, "w1")
+
+        dw_g = gather(dw_tab, k1_l, U32, "dw_g")
+        dw_dealt = sb([P, H], U32, "dw_dealt")
+        nc.vector.tensor_copy(dw_dealt[:].rearrange("p (t u q) -> p u t q", t=4, q=4),
+                              dw_g[:].rearrange("p (u t q) -> p u t q", t=4, q=4))
 
         y_sc = []
         for t in range(TILES):
@@ -144,70 +156,95 @@ def tile_picked_twqsoftbodds_none_p_kernel(tc, x_words, x_scales, w1, w2, gs, d_
             nc.scalar.activation(yy[:], bank[:], ACT.Copy, scale=gs_sb[:, t : t + 1])
             y_sc.append(yy)
 
-        dw_g = gather(dw_tab, k1_l, U32, "dw_g")
-        dw_dealt = sb([P, H], U32, "dw_dealt")
-        nc.vector.tensor_copy(dw_dealt[:].rearrange("p (t u q) -> p u t q", t=4, q=4),
-                              dw_g[:].rearrange("p (u t q) -> p u t q", t=4, q=4))
-
-        ex = [sb([P, S], F32, f"ex{t}") for t in range(TILES)]
         ex_twin = [sb([P, S], F32, f"ex_twin{t}") for t in range(TILES)]
-        h_sb = {t: sb([P, S], F32, f"h_sb{t}") for t in SCALAR_GATHER_TILES}
+        h_sb = w2_raw + w1_raw
         fourth = [sb([P, S], F32, f"fourth{t}") for t in range(TILES)]
 
-        z = [sb([P, 4, width], F32, f"z{i}") for i, (first, width) in enumerate(Z_PIECES)]
-        for i, (first, width) in enumerate(Z_PIECES):
-            for t in range(TILES):
-                nc.vector.tensor_tensor(z[i][:, t, :], y_sc[t][:].indirect(n1_l[:, first // 16 : (first + width) // 16]),
-                                        prod[t][:, first : first + width], ALU.subtract)
         last = len(Z_PIECES) - 1
         for i, (first, width) in enumerate(Z_PIECES):
             piece = slice(first, first + width)
+            if i == 1:
+                early = ex_window[0][:, S:]
+                late = sb([P, 2 * HALF], F32, "prod_b_late", tag="z0")
+                prod_b = [(early, late)[t // 2][:, (t % 2) * HALF : (t % 2 + 1) * HALF] for t in range(TILES)]
+                for t in range(TILES):
+                    tanh_half(t, 1)
+                    times_lookup(prod_b[t], t, 1)
+                z_rest = sb([P, 4 * HALF], F32, "z_rest", tag="z_grouped0")
+            if i == 0:
+                z = sb([P, 4 * width], F32, "z0")[:]
+            else:
+                z = z_rest[:, 4 * (first - HALF) : 4 * (first - HALF + width)]
+            for t in range(TILES):
+                prod = prod_a[t][:] if i == 0 else prod_b[t][:, first - HALF : first - HALF + width]
+                nc.vector.tensor_tensor(z[:, t * width : (t + 1) * width], y_sc[t][:].indirect(n1_l[:, first // 16 : (first + width) // 16]), prod, ALU.subtract)
             z_grouped = sb([P, 4 * width], BF16, f"z_grouped{i}")
             dst = z_grouped[:].rearrange("p (c i t) -> p c t i", i=4, t=4)
-            src = z[i][:].rearrange("p t (c i) -> p c t i", i=4)
-            if i < last:
+            src = z.rearrange("p (t c i) -> p c t i", t=4, i=4)
+            if i == 0:
                 nc.scalar.copy(dst, src)
             else:
                 nc.vector.tensor_copy(dst, src)
             z_q = quantize(z_grouped, width, f"z{i}")
+            banks = []
             for t in range(TILES):
-                bank = psum.tile([P, width], F32, name=f"h_bank{i}{t}", tag=("first", "second")[i % 2] + f"{t}")
-                product(bank[:], (dw_dealt, ds_placed), t, z_q)
-                nc.scalar.activation(ex[t][:, piece], bank[:], ACT.Exp, scale=EXP_SCALE)
-                if i == last - 1:
-                    nc.sync.dma_start(ex_twin[t][:, : first + width], ex[t][:, : first + width])
-                if i == last:
+                banks.append(psum.tile([P, width], F32, name=f"h_bank{i}{t}", tag=("second", "first")[i % 2] + f"{t}"))
+                product(banks[t][:], (dw_dealt, ds_placed), t, z_q)
+
+            def exponentials(t):
+                nc.scalar.activation(ex[t][:, piece], banks[t][:], ACT.Exp, scale=EXP_SCALE)
+                if i == 0:
                     nc.sync.dma_start(ex_twin[t][:, piece], ex[t][:, piece])
-                if t in SCALAR_GATHER_TILES:
-                    nc.scalar.copy(h_sb[t][:, piece], bank[:])
-                    if i == last:
-                        for g in range(2):
-                            nc.scalar.activation(fourth[t][:, cols(g)], h_sb[t][:].indirect(entries(n4_l, g)), ACT.Exp, scale=EXP_SCALE)
+                elif t < DIRECT_TWINS:
+                    nc.scalar.activation(ex_twin[t][:, piece], banks[t][:], ACT.Exp, scale=EXP_SCALE)
+                elif i == last:
+                    nc.sync.dma_start(ex_twin[t][:, HALF:], ex[t][:, HALF:])
+
+            def fourth_term(t):
+                nc.scalar.activation(fourth[t][:], h_sb[t][:].indirect(n4_l[:]), ACT.Exp, scale=EXP_SCALE)
+
+            if i < last:
+                for t in range(TILES):
+                    exponentials(t)
+                    nc.scalar.copy(h_sb[t][:, piece], banks[t][:])
+            else:
+                for t in range(1, TILES):
+                    nc.vector.tensor_copy(h_sb[t][:, piece], banks[t][:])
+                for t in range(DIRECT_TWINS):
+                    exponentials(t)
+                nc.scalar.copy(h_sb[0][:, piece], banks[0][:])
+                fourth_term(0)
+                for t in range(DIRECT_TWINS, TILES):
+                    exponentials(t)
+                for t in range(1, TILES):
+                    fourth_term(t)
 
         sums = [sb([P, 2, S], F32, f"sums{t}") for t in range(TILES)]
 
         def denominator(t):
-            if t not in SCALAR_GATHER_TILES:
-                for g in range(2):
-                    nc.vector.tensor_copy(fourth[t][:, cols(g)], ex[t][:].indirect(entries(n4_l, g)))
-            for g in range(2):
-                nc.vector.tensor_tensor(sums[t][:, 1, cols(g)], ex[t][:].indirect(entries(n5_l, g)), fourth[t][:, cols(g)], ALU.add)
+            nc.vector.tensor_tensor(sums[t][:, 1, :], ex_window[t][:].indirect(n5_l[:]), fourth[t][:], ALU.add)
 
         def numerator(t):
-            for g in range(2):
-                nc.vector.tensor_tensor(sums[t][:, 0, cols(g)], ex[t][:].indirect(entries(n3_l, g)), ex_twin[t][:, cols(g)], ALU.add)
+            nc.vector.tensor_tensor(sums[t][:, 0, :], ex_window[t][:].indirect(n3_l[:]), ex_twin[t][:], ALU.add)
 
-        def finish(t):
-            logs = sb([P, 2, S], F32, f"logs{t}")
-            nc.scalar.activation(logs[:], sums[t][:], ACT.Ln)
-            res = sb([P, S], F32, f"res{t}")
-            nc.vector.tensor_tensor(res[:], logs[:, 0, :], logs[:, 1, :], ALU.subtract)
-            nc.sync.dma_start(out.rearrange("(u t q) n -> t u q n", t=4, q=4)[t], res[:])
+        out_rows = out.rearrange("(u t q) n -> t u q n", t=4, q=4)
 
-        denominator(0)
-        for t in range(TILES):
-            if t + 1 < TILES:
-                denominator(t + 1)
+        logs = sb([P, TILES, 2, S], F32, "logs", tag="w1_raw1")
+
+        def finish(t, part, name):
+            width = part.stop - part.start
+            nc.scalar.activation(logs[:, t, :, part], sums[t][:, :, part], ACT.Ln)
+            res = sb([P, width], F32, "res" + name)
+            nc.vector.tensor_tensor(res[:], logs[:, t, 0, part], logs[:, t, 1, part], ALU.subtract)
+            nc.sync.dma_start(out_rows[t][:, :, part], res[:])
+
+        for t in range(DIRECT_TWINS):
             numerator(t)
         for t in range(TILES):
-            finish(t)
+            denominator(t)
+            if t >= DIRECT_TWINS:
+                numerator(t)
+        for t in range(TILES - 1):
+            finish(t, slice(0, S), f"{t}")
+        for g in range(2):
+            finish(TILES - 1, cols(g), f"last{g}")

from contextlib import ExitStack

import concourse.mybir as mybir

F32 = mybir.dt.float32
BF16 = mybir.dt.bfloat16
U32 = mybir.dt.uint32
I32 = mybir.dt.int32
U16 = mybir.dt.uint16
U8 = mybir.dt.uint8
FP8X4 = mybir.dt.float8_e4m3fn_x4
ACT = mybir.ActivationFunctionType
ALU = mybir.AluOpType

P = 128
K, T, S, H, G = 512, 1024, 512, 512, 2048
TILES = 4
HALF = S // 2
FLOPS = 3 * 2 * K * H * S
EXP_SCALE = 0.5 * 0.0625
DIRECT_TWINS = 2
Z_PIECES = ((0, 256), (256, 128), (384, 128))


def tile_picked_twqsoftbodds_none_p_kernel(tc, x_words, x_scales, w1, w2, gs, d_words, d_scales, offs, two, n1, n2, k1, n3, n4, n5, out):
    nc = tc.nc
    with ExitStack() as ctx:
        lists = ctx.enter_context(tc.tile_pool(name="lists", bufs=1))
        keep = ctx.enter_context(tc.tile_pool(name="keep", bufs=1))
        psum = ctx.enter_context(tc.psum_pool(name="psum", bufs=1))

        def load_list(src, name):
            t = lists.tile([P, S // 16], U16, name=name)
            nc.sync.dma_start(t[:], src)
            return t

        def sb(shape, dtype, name, tag=None):
            return keep.tile(shape, dtype, name=name, tag=tag or name, align_bytes=64)

        def load_weight_half(w, h, name):
            raw = sb([P, 4 * HALF], F32, name)
            nc.sync.dma_start(raw[:].rearrange("p (j c) -> p j c", j=4), w.rearrange("(p j) c -> p j c", j=4)[:, :, h * HALF : (h + 1) * HALF])
            return raw

        def cols(h):
            return slice(h * HALF, (h + 1) * HALF)

        def entries(lst, h):
            return lst[:, h * (HALF // 16) : (h + 1) * (HALF // 16)]

        xs_tab = sb([P, T], U8, "xs_tab")

        def load_x_scales(q):
            (nc.sync, nc.scalar)[q // 2].dma_start(
                xs_tab[32 * q : 32 * q + 32, :].bitcast(I32),
                x_scales[0, 4 * q : 4 * q + 4, :].bitcast(I32).unsqueeze(0).to_broadcast([8, 4, T // 4]),
            )

        two_l = load_list(two, "two_l")
        for q in range(4):
            load_x_scales(q)
        xw_tab = sb([P, T], U32, "xw_tab")
        nc.sync.dma_start(xw_tab[:].bitcast(I32), x_words[0].rearrange("p n t -> p (n t)").bitcast(I32))
        offs_l = load_list(offs, "offs_l")
        w2_raw = [load_weight_half(w2, h, f"w2_raw{h}") for h in range(2)]
        w1_raw = [load_weight_half(w1, 0, "w1_raw0")]
        gs_sb = sb([P, 4], F32, "gs_sb")
        nc.sync.dma_start(gs_sb[:], gs.rearrange("(p t) o -> p (t o)", t=4))
        n2_l = load_list(n2, "n2_l")
        ds_tab = sb([P, G], U8, "ds_tab")
        nc.sync.dma_start(ds_tab[:].bitcast(I32), d_scales[0].bitcast(I32).unsqueeze(1).to_broadcast([16, 8, G // 4]))
        k1_l = load_list(k1, "k1_l")
        w1_raw.append(load_weight_half(w1, 1, "w1_raw1"))
        dw_tab = sb([P, G], U32, "dw_tab")
        nc.sync.dma_start(dw_tab[:].bitcast(I32), d_words[0].rearrange("p n t -> p (n t)").bitcast(I32))
        n1_l = load_list(n1, "n1_l")
        n4_l = load_list(n4, "n4_l")
        n5_l = load_list(n5, "n5_l")
        n3_l = load_list(n3, "n3_l")

        def gather(table, lst, dtype, name):
            g = sb([P, S], dtype, name)
            nc.vector.tensor_copy(g[:], table[:].indirect(lst[:]))
            return g

        def interleave_half(grouped, raw, h):
            view = grouped[:].rearrange("p (t m j) -> p m j t", t=4, j=4)
            nc.scalar.copy(view[:, 64 * h : 64 * h + 64], raw[h][:].rearrange("p (j m t) -> p m j t", j=4, t=4))

        def quantize(src, width, name, calls=1):
            codes = sb([P, width], U32, name + "_codes")
            scales = sb([P, width], U8, name + "_scales")
            step = width // calls
            for c in range(0, width, step):
                nc.vector.quantize_mx(out=codes[:, c : c + step].bitcast(FP8X4), scales=scales[:, c : c + step], in_=src[:, 4 * c : 4 * (c + step)])
            return codes, scales

        def product(bank, lhs, t, rhs):
            m = slice(t * P, (t + 1) * P)
            nc.tensor.matmul_mx(out=bank, lhsT=lhs[0][:, m].bitcast(FP8X4), lhsT_scale=lhs[1][:, m],
                                rhs=rhs[0][:].bitcast(FP8X4), rhs_scale=rhs[1][:], start=True, stop=True)

        xs_two = gather(xs_tab, two_l, U8, "xs_two")
        xw_two = gather(xw_tab, two_l, U32, "xw_two")
        w2_grouped = sb([P, 4 * H], BF16, "w2_grouped")
        w1_grouped = sb([P, 4 * H], BF16, "w1_grouped")
        interleave_half(w2_grouped, w2_raw, 0)
        interleave_half(w2_grouped, w2_raw, 1)
        interleave_half(w1_grouped, w1_raw, 0)
        xs_idx = gather(xs_tab, offs_l, U8, "xs_idx")
        xw_idx = gather(xw_tab, offs_l, U32, "xw_idx")
        w2_q = quantize(w2_grouped, H, "w2", calls=2)

        ds_g = gather(ds_tab, k1_l, U8, "ds_g")
        ds_dealt = sb([P, H], U8, "ds_dealt")
        nc.vector.tensor_copy(ds_dealt[:].bitcast(I32).rearrange("p (t u) -> p u t", t=4),
                              ds_g[:].bitcast(I32).rearrange("p (u t) -> p u t", t=4))
        ds_placed = sb([P, H], U8, "ds_placed")
        nc.vector.memset(ds_placed[:].bitcast(I32), 0)
        for q in range(4):
            nc.sync.dma_start(ds_placed[32 * q : 32 * q + 4, :].bitcast(I32), ds_dealt[32 * q : 32 * q + 32 : 8, :].bitcast(I32))

        ex_window = [sb([P, 2 * S], F32, f"ex_window{t}") for t in range(TILES)]
        ex = [w[:, :S] for w in ex_window]
        tanh_d = [w1_raw[0][:, S:]] + [w[:, S:] for w in ex_window[1:]]
        d_sc = [sb([P, S], F32, f"d_sc{t}") for t in range(TILES)]
        d_banks = []

        def tanh_half(t, h):
            nc.scalar.activation(tanh_d[t][:, cols(h)], d_banks[t][:, cols(h)], ACT.Tanh)

        def times_lookup(dst, t, h):
            nc.vector.tensor_tensor(dst, d_sc[t][:].indirect(entries(n2_l, h)), tanh_d[t][:, cols(h)], ALU.mult)

        prod_a = [sb([P, HALF], F32, f"prod_a{t}") for t in range(TILES)]
        for t in range(TILES):
            d_banks.append(psum.tile([P, S], F32, name=f"d_bank{t}", tag=f"first{t}"))
            product(d_banks[t][:], w2_q, t, (xw_two, xs_two))
            tanh_half(t, 0)
            nc.scalar.activation(d_sc[t][:], d_banks[t][:], ACT.Copy, scale=gs_sb[:, t : t + 1])
            times_lookup(prod_a[t][:], t, 0)
            if t == 0:
                interleave_half(w1_grouped, w1_raw, 1)
                w1_q = quantize(w1_grouped, H, "w1")

        dw_g = gather(dw_tab, k1_l, U32, "dw_g")
        dw_dealt = sb([P, H], U32, "dw_dealt")
        nc.vector.tensor_copy(dw_dealt[:].rearrange("p (t u q) -> p u t q", t=4, q=4),
                              dw_g[:].rearrange("p (u t q) -> p u t q", t=4, q=4))

        y_sc = []
        for t in range(TILES):
            bank = psum.tile([P, S], F32, name=f"y_bank{t}", tag=f"second{t}")
            product(bank[:], w1_q, t, (xw_idx, xs_idx))
            yy = sb([P, S], F32, f"y_sc{t}")
            nc.scalar.activation(yy[:], bank[:], ACT.Copy, scale=gs_sb[:, t : t + 1])
            y_sc.append(yy)

        ex_twin = [sb([P, S], F32, f"ex_twin{t}") for t in range(TILES)]
        h_sb = w2_raw + w1_raw
        fourth = [sb([P, S], F32, f"fourth{t}") for t in range(TILES)]

        last = len(Z_PIECES) - 1
        for i, (first, width) in enumerate(Z_PIECES):
            piece = slice(first, first + width)
            if i == 1:
                early = ex_window[0][:, S:]
                late = sb([P, 2 * HALF], F32, "prod_b_late", tag="z0")
                prod_b = [(early, late)[t // 2][:, (t % 2) * HALF : (t % 2 + 1) * HALF] for t in range(TILES)]
                for t in range(TILES):
                    tanh_half(t, 1)
                    times_lookup(prod_b[t], t, 1)
                z_rest = sb([P, 4 * HALF], F32, "z_rest", tag="z_grouped0")
            if i == 0:
                z = sb([P, 4 * width], F32, "z0")[:]
            else:
                z = z_rest[:, 4 * (first - HALF) : 4 * (first - HALF + width)]
            for t in range(TILES):
                prod = prod_a[t][:] if i == 0 else prod_b[t][:, first - HALF : first - HALF + width]
                nc.vector.tensor_tensor(z[:, t * width : (t + 1) * width], y_sc[t][:].indirect(n1_l[:, first // 16 : (first + width) // 16]), prod, ALU.subtract)
            z_grouped = sb([P, 4 * width], BF16, f"z_grouped{i}")
            dst = z_grouped[:].rearrange("p (c i t) -> p c t i", i=4, t=4)
            src = z.rearrange("p (t c i) -> p c t i", t=4, i=4)
            if i == 0:
                nc.scalar.copy(dst, src)
            else:
                nc.vector.tensor_copy(dst, src)
            z_q = quantize(z_grouped, width, f"z{i}")
            banks = []
            for t in range(TILES):
                banks.append(psum.tile([P, width], F32, name=f"h_bank{i}{t}", tag=("second", "first")[i % 2] + f"{t}"))
                product(banks[t][:], (dw_dealt, ds_placed), t, z_q)

            def exponentials(t):
                nc.scalar.activation(ex[t][:, piece], banks[t][:], ACT.Exp, scale=EXP_SCALE)
                if i == 0:
                    nc.sync.dma_start(ex_twin[t][:, piece], ex[t][:, piece])
                elif t < DIRECT_TWINS:
                    nc.scalar.activation(ex_twin[t][:, piece], banks[t][:], ACT.Exp, scale=EXP_SCALE)
                elif i == last:
                    nc.sync.dma_start(ex_twin[t][:, HALF:], ex[t][:, HALF:])

            def fourth_term(t):
                nc.scalar.activation(fourth[t][:], h_sb[t][:].indirect(n4_l[:]), ACT.Exp, scale=EXP_SCALE)

            if i < last:
                for t in range(TILES):
                    exponentials(t)
                    nc.scalar.copy(h_sb[t][:, piece], banks[t][:])
            else:
                for t in range(1, TILES):
                    nc.vector.tensor_copy(h_sb[t][:, piece], banks[t][:])
                for t in range(DIRECT_TWINS):
                    exponentials(t)
                nc.scalar.copy(h_sb[0][:, piece], banks[0][:])
                fourth_term(0)
                for t in range(DIRECT_TWINS, TILES):
                    exponentials(t)
                for t in range(1, TILES):
                    fourth_term(t)

        sums = [sb([P, 2, S], F32, f"sums{t}") for t in range(TILES)]

        def denominator(t):
            nc.vector.tensor_tensor(sums[t][:, 1, :], ex_window[t][:].indirect(n5_l[:]), fourth[t][:], ALU.add)

        def numerator(t):
            nc.vector.tensor_tensor(sums[t][:, 0, :], ex_window[t][:].indirect(n3_l[:]), ex_twin[t][:], ALU.add)

        out_rows = out.rearrange("(u t q) n -> t u q n", t=4, q=4)

        logs = sb([P, TILES, 2, S], F32, "logs", tag="w1_raw1")

        def finish(t, part, name):
            width = part.stop - part.start
            nc.scalar.activation(logs[:, t, :, part], sums[t][:, :, part], ACT.Ln)
            res = sb([P, width], F32, "res" + name)
            nc.vector.tensor_tensor(res[:], logs[:, t, 0, part], logs[:, t, 1, part], ALU.subtract)
            nc.sync.dma_start(out_rows[t][:, :, part], res[:])

        for t in range(DIRECT_TWINS):
            numerator(t)
        for t in range(TILES):
            denominator(t)
            if t >= DIRECT_TWINS:
                numerator(t)
        for t in range(TILES - 1):
            finish(t, slice(0, S), f"{t}")
        for g in range(2):
            finish(TILES - 1, cols(g), f"last{g}")
